import numpy as np
import ml_dtypes


def mxq(x, axis, fmt="e4m3"):
    dtype, down = {"e4m3": (ml_dtypes.float8_e4m3fn, 7), "e5m2": (ml_dtypes.float8_e5m2, 14)}[fmt]
    v = np.moveaxis(np.asarray(x, np.float32).astype(ml_dtypes.bfloat16).astype(np.float64), axis, -1)
    blocks = v.reshape(v.shape[:-1] + (-1, 32))
    amax = np.abs(blocks).max(-1, keepdims=True)
    byte = np.maximum(np.where(amax > 0, np.frexp(amax)[1] - 1 + 127, 0) - down, 1)
    scale = np.exp2(byte - 127.0)
    codes = (blocks / scale).astype(np.float32).astype(dtype).astype(np.float64)
    return np.moveaxis((codes * scale).reshape(v.shape), -1, axis)


WIDE = False


def mx_kscale(k):
    if not WIDE:
        return np.ones(k)
    levels = np.array([10, -10, 5, -5, 0])
    if k % 512:
        return np.exp2(np.random.permutation(np.resize(levels, k // 32))).repeat(32)
    a = np.empty((k // 512, 16))
    for p in range(k // 512):
        a[p, :8] = np.random.permutation(np.resize(levels, 8))
        for g in range(8):
            far = levels[np.abs(levels - a[p, g]) >= 10]
            a[p, g + 8] = far[np.random.randint(len(far))]
    return np.exp2(a.ravel()).repeat(32)


def f64(x):
    return np.asarray(x).astype(np.float64)


def striped(idx):
    return np.tile(np.asarray(idx).reshape(-1, 16).T, (8, 1)).astype(np.uint16)


def unstriped(offs):
    return offs[:16].T.reshape(-1).astype(np.int64)


E2M1 = np.array([0.0, 0.5, 1.0, 1.5, 2.0, 3.0, 4.0, 6.0, -0.0, -0.5, -1.0, -1.5, -2.0, -3.0, -4.0, -6.0])


def pack_weight(w, fmt):
    k, n = w.shape
    w = f64(np.asarray(w, np.float32).astype(ml_dtypes.bfloat16)).reshape(k // 32, 32, n)
    amax = np.abs(w).max(1)
    if fmt == "e4m3":
        byte = np.frexp(amax)[1] - 1 + 127 - 7
    else:
        mant, ex = np.frexp(amax / 6.0)
        byte = np.where(mant > 0.5, ex, ex - 1) + 127
    byte = np.clip(np.where(amax > 0, byte, 1), 1, 254)
    scaled = (w * np.exp2(127.0 - byte)[:, None, :]).reshape(k, n).astype(np.float32)
    by_word = np.ascontiguousarray(scaled.reshape(k // 512, 128, 4, n).transpose(0, 1, 3, 2))
    if fmt == "e4m3":
        words = by_word.astype(ml_dtypes.float8_e4m3fn).view(np.uint8)
    else:
        c = by_word.astype(ml_dtypes.float4_e2m1fn).view(np.uint8) & 0xF
        words = (c[..., 0::2] | (c[..., 1::2] << 4)).reshape(k // 512, 128, 2 * n)
    return np.ascontiguousarray(words), np.ascontiguousarray(byte.astype(np.uint8).reshape(k // 512, 16, n))


def unpack_weight(words, scales, fmt):
    g, _, n = scales.shape
    words = np.ascontiguousarray(words).reshape(g, 128, n, -1)
    if fmt == "e4m3":
        vals = words.view(ml_dtypes.float8_e4m3fn).astype(np.float64)
    else:
        nib = np.empty((g, 128, n, 4), np.uint8)
        nib[..., 0::2] = words & 0xF
        nib[..., 1::2] = words >> 4
        vals = E2M1[nib]
    vals = vals * np.repeat(np.exp2(scales.astype(np.float64) - 127.0), 8, axis=1)[..., None]
    return vals.transpose(0, 1, 3, 2).reshape(g * 512, n)


def softplus(v):
    return np.log(1.0 + np.exp(v))


B, N, T, D, NQ = 1, 512, 2048, 512, 256
SEG = 32


def setup_inputs():
    n = np.random.standard_normal
    idx = np.random.permutation(T)[:B * N]
    s = mx_kscale(D)[:, None]
    kp = pack_weight(n((D, T)) / s, "e4m3")
    return {
        "qT": (n((B, D, NQ)) * s * (1.00 / np.sqrt(D))).astype(np.float32),
        "k_words": kp[0],
        "k_scales": kp[1],
        "lq": np.tile(np.random.uniform(-1.0, 1.0, 2048), (128, 1)).astype(np.float32),
        "offs": striped(idx),
    }


def reference(qT, k_words, k_scales, lq, offs):
    idx = unstriped(offs)
    pick = lambda x, which: x[:, which].reshape(x.shape[0], B, -1).transpose(1, 0, 2)
    k = unpack_weight(k_words, k_scales, "e4m3")
    kg = pick(k, idx)
    qq = mxq(f64(qT), 1, "e4m3")
    a = qq.transpose(0, 2, 1) @ kg
    y = softplus(a - pick(f64(lq), idx)[:, :1, :]).reshape(B, NQ, N // SEG, SEG).sum(-1)
    return y

@@ -1,0 +1,154 @@
+import math
+from contextlib import ExitStack
+
+import concourse.mybir as mybir
+from concourse.masks import make_identity
+
+F32 = mybir.dt.float32
+BF16 = mybir.dt.bfloat16
+I32 = mybir.dt.int32
+U32 = mybir.dt.uint32
+U16 = mybir.dt.uint16
+U8 = mybir.dt.uint8
+FP8X4 = mybir.dt.float8_e4m3fn_x4
+ALU = mybir.AluOpType
+ACT = mybir.ActivationFunctionType
+AX = mybir.AxisListType
+
+P = 128
+T = 2048
+N = 512
+NQ = 256
+D = 512
+RUNS = 16
+HALF_RUN = 16
+CAP = 20.0
+PITCH = 20
+FLOPS = 2 * NQ * N * D
+BYTES = D * NQ * 4 + P * T * 4 + 16 * T + T * 4 + P * (N // 16) * 2 + NQ * RUNS * 4
+
+
+def tile_attend_nce_topk_kernel(tc, qT, k_words, k_scales, lq, offs, out):
+    nc = tc.nc
+    with ExitStack() as ctx:
+        held = ctx.enter_context(tc.tile_pool(name="held", bufs=1))
+        psum = ctx.enter_context(tc.psum_pool(name="psum", bufs=1))
+
+        offsets = held.tile([P, N // 16], U16, name="offsets")
+        lq_pool = held.tile([P, T], F32, name="lq_pool")
+        scale_pool = held.tile([P, T // 4], I32, name="scale_pool")
+        word_pool = held.tile([P, T], I32, name="word_pool")
+        q_raw = held.tile([P, 4, NQ], F32, name="q_raw")
+
+        nc.vector.memset(scale_pool[:], 0)
+        nc.scalar.dma_start(out=q_raw[:], in_=qT[0].rearrange("(p j) w -> p j w", j=4))
+        nc.sync.dma_start(offsets[:], offs)
+        nc.sync.dma_start(out=lq_pool[P - 1 : P, :], in_=lq[0:1, :])
+        scale_rows = k_scales[0].bitcast(I32)
+        for quad in range(4):
+            nc.sync.dma_start(out=scale_pool[32 * quad : 32 * quad + 4, :], in_=scale_rows[4 * quad : 4 * quad + 4, :])
+        nc.sync.dma_start(out=word_pool[:], in_=k_words[0].rearrange("p t r -> p (t r)").bitcast(I32))
+        nc.vector.memset(lq_pool[0 : P - 1, :], 0.0)
+
+        ident = held.tile([P, P], F32, name="ident")
+        make_identity(nc, ident[:])
+
+        lq_listed = held.tile([P, N], F32, name="lq_listed")
+        nc.vector.tensor_copy(lq_listed[:], lq_pool[:].indirect(offsets[:]))
+        scale_listed = held.tile([P, N], U8, name="scale_listed")
+        nc.vector.tensor_copy(scale_listed[:], scale_pool[:].bitcast(U8).indirect(offsets[:]))
+        scale_paired = held.tile([P, N], U8, name="scale_paired", align_bytes=64)
+        nc.vector.tensor_copy(
+            scale_paired[:].bitcast(I32).rearrange("p (t s r) -> p t s r", t=2, s=RUNS),
+            scale_listed[:].bitcast(I32).rearrange("p (s t r) -> p t s r", t=2, s=RUNS),
+        )
+        scale_cols = scale_paired[:]
+
+        q_grouped = held.tile([P, NQ, 4], BF16, name="q_grouped", align_bytes=64)
+        nc.scalar.activation(
+            q_grouped[:].rearrange("p (c i) j -> p c j i", i=4),
+            q_raw[:].rearrange("p j (c i) -> p c j i", i=4),
+            ACT.Copy,
+        )
+        q_codes = held.tile([P, NQ], U32, name="q_codes", align_bytes=64)
+        q_scales = held.tile([P, NQ], U8, name="q_scales", align_bytes=64)
+        nc.vector.quantize_mx(
+            out=q_codes[:].bitcast(FP8X4), scales=q_scales[:], in_=q_grouped[:].rearrange("p w j -> p (w j)")
+        )
+
+        lq_paired = held.tile([P, N], F32, name="lq_paired")
+        nc.scalar.activation(
+            lq_paired[:].rearrange("p (t s r) -> p t s r", t=2, s=RUNS),
+            lq_listed[:].rearrange("p (s t r) -> p t s r", t=2, s=RUNS),
+            ACT.Copy,
+        )
+        lq_cols = lq_paired[:]
+        lq_turned = psum.tile([P, 4, P], F32, name="lq_turned")
+        for blk in range(4):
+            nc.tensor.transpose(lq_turned[:, blk, :], lq_cols[:, blk * P : (blk + 1) * P], ident[:])
+        neg_lq = held.tile([P, 4], F32, name="neg_lq")
+        nc.scalar.activation(neg_lq[:], lq_turned[:, :, P - 1], ACT.Copy, scale=-1.0)
+        knee = held.tile([P, 4], F32, name="knee")
+        nc.scalar.activation(knee[:], lq_turned[:, :, P - 1], ACT.Copy, bias=CAP)
+        knee_sum = held.tile([P, 2], F32, name="knee_sum")
+        nc.gpsimd.tensor_tensor(knee_sum[:], knee[:, 0:2], knee[:, 2:4], ALU.add)
+
+        words = []
+        for h in range(2):
+            listed = held.tile([P, 2, RUNS // 2, HALF_RUN], U32, name=f"words{h}", align_bytes=64)
+            nc.vector.tensor_copy(
+                listed[:].rearrange("p t s r -> p s t r"),
+                word_pool[:].bitcast(U32).indirect(offsets[:, 16 * h : 16 * (h + 1)]),
+            )
+            words.append(listed)
+
+        prod_turned = [psum.tile([P, 2, P], F32, name=f"prod_turned{qb}") for qb in range(2)]
+        over_turned = psum.tile([P, 2, 2, P], F32, name="over_turned")
+        for h in range(2):
+            scores = []
+            expv = held.tile([P, 2, NQ], F32, name=f"expv{h}")
+            for t in range(2):
+                blk = 2 * t + h
+                bank = psum.tile([P, NQ], F32, name=f"scores{h}{t}")
+                nc.tensor.matmul_mx(
+                    out=bank[:],
+                    lhsT=words[h][:].rearrange("p t s r -> p t (s r)")[:, t, :].bitcast(FP8X4),
+                    lhsT_scale=scale_cols[:, blk * P : (blk + 1) * P],
+                    rhs=q_codes[:].bitcast(FP8X4),
+                    rhs_scale=q_scales[:],
+                    start=True,
+                    stop=True,
+                )
+                nc.scalar.activation(expv[:, t, :], bank[:], ACT.Exp, bias=neg_lq[:, blk : blk + 1])
+                scores.append(bank)
+            part = held.tile([P, NQ], F32, name=f"part{h}")
+            over = held.tile([P, NQ], F32, name=f"over{h}")
+            fac = held.tile([P, 2, NQ], F32, name=f"fac{h}")
+            prod = held.tile([P, NQ], F32, name=f"prod{h}")
+            nc.vector.tensor_scalar(
+                part[:], scores[0][:], knee[:, h : h + 1], knee_sum[:, h : h + 1], ALU.max, ALU.subtract
+            )
+            nc.vector.tensor_scalar(fac[:], expv[:], 1.0, 1.0 + math.exp(CAP), ALU.add, ALU.min)
+            nc.vector.scalar_tensor_tensor(over[:], scores[1][:], knee[:, 2 + h : 3 + h], part[:], ALU.max, ALU.add)
+            nc.vector.tensor_tensor(prod[:], fac[:, 0, :], fac[:, 1, :], ALU.mult)
+            for qb in range(2):
+                nc.tensor.transpose(over_turned[:, qb, h, :], over[:, qb * P : (qb + 1) * P], ident[:])
+            for qb in range(2):
+                nc.tensor.transpose(prod_turned[qb][:, h, :], prod[:, qb * P : (qb + 1) * P], ident[:])
+
+        terms = held.tile([P, 2, RUNS, PITCH], F32, name="terms")
+        nc.vector.tensor_reduce(
+            terms[:, :, :, HALF_RUN],
+            over_turned[:].rearrange("p b h (s r) -> p b (h s) r", r=HALF_RUN),
+            AX.X,
+            ALU.add,
+        )
+        for qb in range(2):
+            nc.scalar.activation(
+                terms[:, qb, :, 0:HALF_RUN],
+                prod_turned[qb][:].rearrange("p h (s r) -> p (h s) r", r=HALF_RUN),
+                ACT.Ln,
+            )
+            sums = held.tile([P, RUNS], F32, name=f"sums{qb}")
+            nc.vector.tensor_reduce(sums[:], terms[:, qb, :, 0 : HALF_RUN + 1], AX.X, ALU.add)
+            nc.sync.dma_start(out=out[0, qb * P : (qb + 1) * P, :], in_=sums[:])

@@ -1,4 +1,3 @@
-import math
 from contextlib import ExitStack
 
 import concourse.mybir as mybir
@@ -35,7 +34,7 @@ def tile_attend_nce_topk_kernel(tc, qT, k_words, k_scales, lq, offs, out):
         psum = ctx.enter_context(tc.psum_pool(name="psum", bufs=1))
 
         offsets = held.tile([P, N // 16], U16, name="offsets")
-        lq_pool = held.tile([P, T], F32, name="lq_pool")
+        lq_pool = held.tile([P, T], F32, name="lq_pool", tag="lq_then_q", align_bytes=64)
         scale_pool = held.tile([P, T // 4], I32, name="scale_pool")
         word_pool = held.tile([P, T], I32, name="word_pool")
         q_raw = held.tile([P, 4, NQ], F32, name="q_raw")
@@ -50,6 +49,11 @@ def tile_attend_nce_topk_kernel(tc, qT, k_words, k_scales, lq, offs, out):
         nc.sync.dma_start(out=word_pool[:], in_=k_words[0].rearrange("p t r -> p (t r)").bitcast(I32))
         nc.vector.memset(lq_pool[0 : P - 1, :], 0.0)
 
+        neg_cap = held.tile([P, 1], F32, name="neg_cap")
+        nc.gpsimd.memset(neg_cap[:], -CAP)
+        floor = held.tile([P, 1], F32, name="floor")
+        nc.scalar.activation(floor[:], neg_cap[:], ACT.Sigmoid)
+
         ident = held.tile([P, P], F32, name="ident")
         make_identity(nc, ident[:])
 
@@ -57,12 +61,12 @@ def tile_attend_nce_topk_kernel(tc, qT, k_words, k_scales, lq, offs, out):
         nc.vector.tensor_copy(lq_listed[:], lq_pool[:].indirect(offsets[:]))
         scale_listed = held.tile([P, N], U8, name="scale_listed")
         nc.vector.tensor_copy(scale_listed[:], scale_pool[:].bitcast(U8).indirect(offsets[:]))
-        scale_paired = held.tile([P, N], U8, name="scale_paired", align_bytes=64)
-        nc.vector.tensor_copy(
-            scale_paired[:].bitcast(I32).rearrange("p (t s r) -> p t s r", t=2, s=RUNS),
-            scale_listed[:].bitcast(I32).rearrange("p (s t r) -> p t s r", t=2, s=RUNS),
+        lq_paired = held.tile([P, N], F32, name="lq_paired")
+        nc.scalar.activation(
+            lq_paired[:].rearrange("p (t s r) -> p t s r", t=2, s=RUNS),
+            lq_listed[:].rearrange("p (s t r) -> p t s r", t=2, s=RUNS),
+            ACT.Copy,
         )
-        scale_cols = scale_paired[:]
 
         q_grouped = held.tile([P, NQ, 4], BF16, name="q_grouped", align_bytes=64)
         nc.scalar.activation(
@@ -70,85 +74,94 @@ def tile_attend_nce_topk_kernel(tc, qT, k_words, k_scales, lq, offs, out):
             q_raw[:].rearrange("p j (c i) -> p c j i", i=4),
             ACT.Copy,
         )
-        q_codes = held.tile([P, NQ], U32, name="q_codes", align_bytes=64)
+        q_codes = held.tile([P, NQ], U32, name="q_codes", tag="lq_then_q", align_bytes=64)
         q_scales = held.tile([P, NQ], U8, name="q_scales", align_bytes=64)
         nc.vector.quantize_mx(
             out=q_codes[:].bitcast(FP8X4), scales=q_scales[:], in_=q_grouped[:].rearrange("p w j -> p (w j)")
         )
 
-        lq_paired = held.tile([P, N], F32, name="lq_paired")
-        nc.scalar.activation(
-            lq_paired[:].rearrange("p (t s r) -> p t s r", t=2, s=RUNS),
-            lq_listed[:].rearrange("p (s t r) -> p t s r", t=2, s=RUNS),
-            ACT.Copy,
+        scale_paired = held.tile([P, N], U8, name="scale_paired", align_bytes=64)
+        nc.vector.tensor_copy(
+            scale_paired[:].bitcast(I32).rearrange("p (t s r) -> p t s r", t=2, s=RUNS),
+            scale_listed[:].bitcast(I32).rearrange("p (s t r) -> p t s r", t=2, s=RUNS),
         )
-        lq_cols = lq_paired[:]
+        scale_cols = scale_paired[:]
+
         lq_turned = psum.tile([P, 4, P], F32, name="lq_turned")
         for blk in range(4):
-            nc.tensor.transpose(lq_turned[:, blk, :], lq_cols[:, blk * P : (blk + 1) * P], ident[:])
-        neg_lq = held.tile([P, 4], F32, name="neg_lq")
-        nc.scalar.activation(neg_lq[:], lq_turned[:, :, P - 1], ACT.Copy, scale=-1.0)
+            nc.tensor.transpose(lq_turned[:, blk, :], lq_paired[:, blk * P : (blk + 1) * P], ident[:])
+        lq_col = held.tile([P, 4], F32, name="lq_col")
+        nc.scalar.activation(lq_col[:], lq_turned[:, :, P - 1], ACT.Copy)
         knee = held.tile([P, 4], F32, name="knee")
         nc.scalar.activation(knee[:], lq_turned[:, :, P - 1], ACT.Copy, bias=CAP)
         knee_sum = held.tile([P, 2], F32, name="knee_sum")
-        nc.gpsimd.tensor_tensor(knee_sum[:], knee[:, 0:2], knee[:, 2:4], ALU.add)
-
-        words = []
         for h in range(2):
-            listed = held.tile([P, 2, RUNS // 2, HALF_RUN], U32, name=f"words{h}", align_bytes=64)
+            nc.scalar.activation(knee_sum[:, h : h + 1], knee[:, 2 + h : 3 + h], ACT.Identity, bias=knee[:, h : h + 1])
+
+        words = held.tile([P, 2, 2, RUNS // 2, HALF_RUN], U32, name="words", align_bytes=64)
+        for h in range(2):
             nc.vector.tensor_copy(
-                listed[:].rearrange("p t s r -> p s t r"),
+                words[:, h].rearrange("p t s r -> p s t r"),
                 word_pool[:].bitcast(U32).indirect(offsets[:, 16 * h : 16 * (h + 1)]),
             )
-            words.append(listed)
 
-        prod_turned = [psum.tile([P, 2, P], F32, name=f"prod_turned{qb}") for qb in range(2)]
-        over_turned = psum.tile([P, 2, 2, P], F32, name="over_turned")
+        scores = {}
+        sig = {}
         for h in range(2):
-            scores = []
-            expv = held.tile([P, 2, NQ], F32, name=f"expv{h}")
             for t in range(2):
                 blk = 2 * t + h
-                bank = psum.tile([P, NQ], F32, name=f"scores{h}{t}")
+                bank = psum.tile([P, NQ], F32, name=f"scores{h}{t}", tag=f"bank{h}{t}")
                 nc.tensor.matmul_mx(
                     out=bank[:],
-                    lhsT=words[h][:].rearrange("p t s r -> p t (s r)")[:, t, :].bitcast(FP8X4),
+                    lhsT=words[:].rearrange("p h t s r -> p h t (s r)")[:, h, t, :].bitcast(FP8X4),
                     lhsT_scale=scale_cols[:, blk * P : (blk + 1) * P],
                     rhs=q_codes[:].bitcast(FP8X4),
                     rhs_scale=q_scales[:],
                     start=True,
                     stop=True,
                 )
-                nc.scalar.activation(expv[:, t, :], bank[:], ACT.Exp, bias=neg_lq[:, blk : blk + 1])
-                scores.append(bank)
-            part = held.tile([P, NQ], F32, name=f"part{h}")
-            over = held.tile([P, NQ], F32, name=f"over{h}")
-            fac = held.tile([P, 2, NQ], F32, name=f"fac{h}")
-            prod = held.tile([P, NQ], F32, name=f"prod{h}")
-            nc.vector.tensor_scalar(
-                part[:], scores[0][:], knee[:, h : h + 1], knee_sum[:, h : h + 1], ALU.max, ALU.subtract
-            )
-            nc.vector.tensor_scalar(fac[:], expv[:], 1.0, 1.0 + math.exp(CAP), ALU.add, ALU.min)
-            nc.vector.scalar_tensor_tensor(over[:], scores[1][:], knee[:, 2 + h : 3 + h], part[:], ALU.max, ALU.add)
-            nc.vector.tensor_tensor(prod[:], fac[:, 0, :], fac[:, 1, :], ALU.mult)
-            for qb in range(2):
-                nc.tensor.transpose(over_turned[:, qb, h, :], over[:, qb * P : (qb + 1) * P], ident[:])
-            for qb in range(2):
-                nc.tensor.transpose(prod_turned[qb][:, h, :], prod[:, qb * P : (qb + 1) * P], ident[:])
+                s = held.tile([P, NQ], F32, name=f"sig{h}{t}")
+                nc.scalar.activation(s[:], bank[:], ACT.Sigmoid, bias=lq_col[:, blk : blk + 1], scale=-1.0)
+                scores[h, t] = bank
+                sig[h, t] = s
 
         terms = held.tile([P, 2, RUNS, PITCH], F32, name="terms")
-        nc.vector.tensor_reduce(
-            terms[:, :, :, HALF_RUN],
-            over_turned[:].rearrange("p b h (s r) -> p b (h s) r", r=HALF_RUN),
-            AX.X,
-            ALU.add,
-        )
-        for qb in range(2):
+        turned = []
+        excess = []
+        for h in range(2):
+            first = held.tile([P, NQ], F32, name=f"first{h}")
+            nc.vector.tensor_scalar(first[:], sig[h, 0][:], floor[:], None, ALU.max)
+            part = held.tile([P, NQ], F32, name=f"part{h}")
+            nc.vector.tensor_scalar(
+                part[:], scores[h, 0][:], knee[:, h : h + 1], knee_sum[:, h : h + 1], ALU.max, ALU.subtract
+            )
+            prod = held.tile([P, NQ], F32, name=f"prod{h}")
+            nc.vector.scalar_tensor_tensor(prod[:], sig[h, 1][:], floor[:], first[:], ALU.max, ALU.mult)
+            over = held.tile([P, NQ], F32, name=f"over{h}")
+            nc.vector.scalar_tensor_tensor(over[:], scores[h, 1][:], knee[:, 2 + h : 3 + h], part[:], ALU.max, ALU.add)
+            prod_turned = psum.tile([P, 2, P], F32, name=f"prod_turned{h}")
+            for qb in range(2):
+                nc.tensor.transpose(prod_turned[:, qb, :], prod[:, qb * P : (qb + 1) * P], ident[:])
+            over_turned = psum.tile([P, 2, P], F32, name=f"over_turned{h}", tag=f"bank{h}0")
+            for qb in range(2):
+                nc.tensor.transpose(over_turned[:, qb, :], over[:, qb * P : (qb + 1) * P], ident[:])
+            turned.append(prod_turned)
+            excess.append(over_turned)
+        for h in range(2):
+            nc.vector.tensor_reduce(
+                terms[:, :, h * (RUNS // 2) : (h + 1) * (RUNS // 2), HALF_RUN],
+                excess[h][:].rearrange("p b (s r) -> p b s r", r=HALF_RUN),
+                AX.X,
+                ALU.add,
+                negate=True,
+            )
+        sums = held.tile([P, 2, RUNS], F32, name="sums")
+        for h in range(2):
+            runs = slice(h * (RUNS // 2), (h + 1) * (RUNS // 2))
             nc.scalar.activation(
-                terms[:, qb, :, 0:HALF_RUN],
-                prod_turned[qb][:].rearrange("p h (s r) -> p (h s) r", r=HALF_RUN),
+                terms[:, :, runs, 0:HALF_RUN],
+                turned[h][:].rearrange("p b (s r) -> p b s r", r=HALF_RUN),
                 ACT.Ln,
             )
-            sums = held.tile([P, RUNS], F32, name=f"sums{qb}")
-            nc.vector.tensor_reduce(sums[:], terms[:, qb, :, 0 : HALF_RUN + 1], AX.X, ALU.add)
-            nc.sync.dma_start(out=out[0, qb * P : (qb + 1) * P, :], in_=sums[:])
+            nc.vector.tensor_reduce(sums[:, :, runs], terms[:, :, runs, 0 : HALF_RUN + 1], AX.X, ALU.add, negate=True)
+        nc.sync.dma_start(out=out[0].rearrange("(b p) r -> p b r", b=2), in_=sums[:])

@@ -34,18 +34,18 @@ def tile_attend_nce_topk_kernel(tc, qT, k_words, k_scales, lq, offs, out):
         psum = ctx.enter_context(tc.psum_pool(name="psum", bufs=1))
 
         offsets = held.tile([P, N // 16], U16, name="offsets")
-        lq_pool = held.tile([P, T], F32, name="lq_pool", tag="lq_then_q", align_bytes=64)
-        scale_pool = held.tile([P, T // 4], I32, name="scale_pool")
+        lq_pool = held.tile([P, T], F32, name="lq_pool", tag="lq_then_scales")
+        scale_pool = held.tile([P, T // 4], I32, name="scale_pool", tag="scales_then_q", align_bytes=64)
         word_pool = held.tile([P, T], I32, name="word_pool")
         q_raw = held.tile([P, 4, NQ], F32, name="q_raw")
 
         nc.vector.memset(scale_pool[:], 0)
-        nc.scalar.dma_start(out=q_raw[:], in_=qT[0].rearrange("(p j) w -> p j w", j=4))
         nc.sync.dma_start(offsets[:], offs)
         nc.sync.dma_start(out=lq_pool[P - 1 : P, :], in_=lq[0:1, :])
         scale_rows = k_scales[0].bitcast(I32)
-        for quad in range(4):
-            nc.sync.dma_start(out=scale_pool[32 * quad : 32 * quad + 4, :], in_=scale_rows[4 * quad : 4 * quad + 4, :])
+        for r in range(4):
+            nc.sync.dma_start(out=scale_pool[r:P:32, :], in_=scale_rows[r:16:4, :])
+        nc.sync.dma_start(out=q_raw[:], in_=qT[0].rearrange("(p j) w -> p j w", j=4))
         nc.sync.dma_start(out=word_pool[:], in_=k_words[0].rearrange("p t r -> p (t r)").bitcast(I32))
         nc.vector.memset(lq_pool[0 : P - 1, :], 0.0)
 
@@ -59,7 +59,7 @@ def tile_attend_nce_topk_kernel(tc, qT, k_words, k_scales, lq, offs, out):
 
         lq_listed = held.tile([P, N], F32, name="lq_listed")
         nc.vector.tensor_copy(lq_listed[:], lq_pool[:].indirect(offsets[:]))
-        scale_listed = held.tile([P, N], U8, name="scale_listed")
+        scale_listed = held.tile([P, N], U8, name="scale_listed", tag="lq_then_scales")
         nc.vector.tensor_copy(scale_listed[:], scale_pool[:].bitcast(U8).indirect(offsets[:]))
         lq_paired = held.tile([P, N], F32, name="lq_paired")
         nc.scalar.activation(
@@ -74,7 +74,7 @@ def tile_attend_nce_topk_kernel(tc, qT, k_words, k_scales, lq, offs, out):
             q_raw[:].rearrange("p j (c i) -> p c j i", i=4),
             ACT.Copy,
         )
-        q_codes = held.tile([P, NQ], U32, name="q_codes", tag="lq_then_q", align_bytes=64)
+        q_codes = held.tile([P, NQ], U32, name="q_codes", tag="scales_then_q", align_bytes=64)
         q_scales = held.tile([P, NQ], U8, name="q_scales", align_bytes=64)
         nc.vector.quantize_mx(
             out=q_codes[:].bitcast(FP8X4), scales=q_scales[:], in_=q_grouped[:].rearrange("p w j -> p (w j)")

@@ -37,37 +37,32 @@ def tile_attend_nce_topk_kernel(tc, qT, k_words, k_scales, lq, offs, out):
         lq_pool = held.tile([P, T], F32, name="lq_pool", tag="lq_then_scales")
         scale_pool = held.tile([P, T // 4], I32, name="scale_pool", tag="scales_then_q", align_bytes=64)
         word_pool = held.tile([P, T], I32, name="word_pool")
-        q_raw = held.tile([P, 4, NQ], F32, name="q_raw")
+        q_raw = held.tile([P, 4, NQ], F32, name="q_raw", tag="q_then_lq")
 
         nc.vector.memset(scale_pool[:], 0)
         nc.sync.dma_start(offsets[:], offs)
         nc.sync.dma_start(out=lq_pool[P - 1 : P, :], in_=lq[0:1, :])
         scale_rows = k_scales[0].bitcast(I32)
         for r in range(4):
-            nc.sync.dma_start(out=scale_pool[r:P:32, :], in_=scale_rows[r:16:4, :])
+            queue = nc.sync if r % 2 == 0 else nc.scalar
+            queue.dma_start(out=scale_pool[r:P:32, :], in_=scale_rows[r:16:4, :])
         nc.sync.dma_start(out=q_raw[:], in_=qT[0].rearrange("(p j) w -> p j w", j=4))
         nc.sync.dma_start(out=word_pool[:], in_=k_words[0].rearrange("p t r -> p (t r)").bitcast(I32))
-        nc.vector.memset(lq_pool[0 : P - 1, :], 0.0)
 
         neg_cap = held.tile([P, 1], F32, name="neg_cap")
-        nc.gpsimd.memset(neg_cap[:], -CAP)
+        nc.vector.memset(neg_cap[:], -CAP)
         floor = held.tile([P, 1], F32, name="floor")
         nc.scalar.activation(floor[:], neg_cap[:], ACT.Sigmoid)
 
+        nc.vector.memset(lq_pool[0 : P - 1, :], 0.0)
         ident = held.tile([P, P], F32, name="ident")
-        make_identity(nc, ident[:])
+        nc.vector.memset(ident[:], 0.0)
+        make_identity(nc, ident[:], nomemset=True)
 
         lq_listed = held.tile([P, N], F32, name="lq_listed")
         nc.vector.tensor_copy(lq_listed[:], lq_pool[:].indirect(offsets[:]))
         scale_listed = held.tile([P, N], U8, name="scale_listed", tag="lq_then_scales")
         nc.vector.tensor_copy(scale_listed[:], scale_pool[:].bitcast(U8).indirect(offsets[:]))
-        lq_paired = held.tile([P, N], F32, name="lq_paired")
-        nc.scalar.activation(
-            lq_paired[:].rearrange("p (t s r) -> p t s r", t=2, s=RUNS),
-            lq_listed[:].rearrange("p (s t r) -> p t s r", t=2, s=RUNS),
-            ACT.Copy,
-        )
-
         q_grouped = held.tile([P, NQ, 4], BF16, name="q_grouped", align_bytes=64)
         nc.scalar.activation(
             q_grouped[:].rearrange("p (c i) j -> p c j i", i=4),
@@ -86,6 +81,13 @@ def tile_attend_nce_topk_kernel(tc, qT, k_words, k_scales, lq, offs, out):
             scale_listed[:].bitcast(I32).rearrange("p (s t r) -> p t s r", t=2, s=RUNS),
         )
         scale_cols = scale_paired[:]
+
+        lq_paired = held.tile([P, N], F32, name="lq_paired", tag="q_then_lq")
+        nc.scalar.activation(
+            lq_paired[:].rearrange("p (t s r) -> p t s r", t=2, s=RUNS),
+            lq_listed[:].rearrange("p (s t r) -> p t s r", t=2, s=RUNS),
+            ACT.Copy,
+        )
 
         lq_turned = psum.tile([P, 4, P], F32, name="lq_turned")
         for blk in range(4):

@@ -23,6 +23,7 @@ RUNS = 16
 HALF_RUN = 16
 CAP = 20.0
 PITCH = 20
+ROW0 = 48
 FLOPS = 2 * NQ * N * D
 BYTES = D * NQ * 4 + P * T * 4 + 16 * T + T * 4 + P * (N // 16) * 2 + NQ * RUNS * 4
 
@@ -34,18 +35,14 @@ def tile_attend_nce_topk_kernel(tc, qT, k_words, k_scales, lq, offs, out):
         psum = ctx.enter_context(tc.psum_pool(name="psum", bufs=1))
 
         offsets = held.tile([P, N // 16], U16, name="offsets")
-        lq_pool = held.tile([P, T], F32, name="lq_pool", tag="lq_then_scales")
-        scale_pool = held.tile([P, T // 4], I32, name="scale_pool", tag="scales_then_q", align_bytes=64)
+        lq_pool = held.tile([P, T], F32, name="lq_pool", tag="lq_then_q", align_bytes=64)
+        scale_pool = held.tile([P, T // 4], I32, name="scale_pool", tag="scales_then_lq")
         word_pool = held.tile([P, T], I32, name="word_pool")
         q_raw = held.tile([P, 4, NQ], F32, name="q_raw", tag="q_then_lq")
 
-        nc.vector.memset(scale_pool[:], 0)
         nc.sync.dma_start(offsets[:], offs)
-        nc.sync.dma_start(out=lq_pool[P - 1 : P, :], in_=lq[0:1, :])
-        scale_rows = k_scales[0].bitcast(I32)
-        for r in range(4):
-            queue = nc.sync if r % 2 == 0 else nc.scalar
-            queue.dma_start(out=scale_pool[r:P:32, :], in_=scale_rows[r:16:4, :])
+        nc.sync.dma_start(out=scale_pool[ROW0 : ROW0 + 16, :], in_=k_scales[0].bitcast(I32))
+        nc.scalar.dma_start(out=lq_pool[P - 1 : P, :], in_=lq[0:1, :])
         nc.sync.dma_start(out=q_raw[:], in_=qT[0].rearrange("(p j) w -> p j w", j=4))
         nc.sync.dma_start(out=word_pool[:], in_=k_words[0].rearrange("p t r -> p (t r)").bitcast(I32))
 
@@ -54,44 +51,55 @@ def tile_attend_nce_topk_kernel(tc, qT, k_words, k_scales, lq, offs, out):
         floor = held.tile([P, 1], F32, name="floor")
         nc.scalar.activation(floor[:], neg_cap[:], ACT.Sigmoid)
 
+        nc.vector.memset(scale_pool[0:ROW0, :], 0)
+        nc.vector.memset(scale_pool[ROW0 + 16 : P, :], 0)
+        scale_plane = held.tile([P, N], U8, name="scale_plane", align_bytes=64)
+        nc.vector.memset(scale_plane[:].bitcast(I32), 0)
         nc.vector.memset(lq_pool[0 : P - 1, :], 0.0)
         ident = held.tile([P, P], F32, name="ident")
         nc.vector.memset(ident[:], 0.0)
         make_identity(nc, ident[:], nomemset=True)
 
-        lq_listed = held.tile([P, N], F32, name="lq_listed")
-        nc.vector.tensor_copy(lq_listed[:], lq_pool[:].indirect(offsets[:]))
-        scale_listed = held.tile([P, N], U8, name="scale_listed", tag="lq_then_scales")
+        scale_listed = held.tile([P, N], U8, name="scale_listed")
         nc.vector.tensor_copy(scale_listed[:], scale_pool[:].bitcast(U8).indirect(offsets[:]))
+        scale_paired = held.tile([P, N], U8, name="scale_paired")
+        nc.vector.tensor_copy(
+            scale_paired[:].bitcast(I32).rearrange("p (t s r) -> p t s r", t=2, s=RUNS),
+            scale_listed[:].bitcast(I32).rearrange("p (s t r) -> p t s r", t=2, s=RUNS),
+        )
+        for r in range(4):
+            nc.sync.dma_start(
+                out=scale_plane[:].bitcast(I32)[r:P:32, :], in_=scale_paired[:].bitcast(I32)[ROW0 + r : ROW0 + 16 : 4, :]
+            )
+        scale_cols = scale_plane[:]
+
+        lq_listed = held.tile([P, 2, N // 2], F32, name="lq_listed", tag="scales_then_lq")
+        for h in range(2):
+            nc.vector.tensor_copy(lq_listed[:, h, :], lq_pool[:].indirect(offsets[:, 16 * h : 16 * (h + 1)]))
+
         q_grouped = held.tile([P, NQ, 4], BF16, name="q_grouped", align_bytes=64)
         nc.scalar.activation(
             q_grouped[:].rearrange("p (c i) j -> p c j i", i=4),
             q_raw[:].rearrange("p j (c i) -> p c j i", i=4),
             ACT.Copy,
         )
-        q_codes = held.tile([P, NQ], U32, name="q_codes", tag="scales_then_q", align_bytes=64)
+        q_codes = held.tile([P, NQ], U32, name="q_codes", tag="lq_then_q", align_bytes=64)
         q_scales = held.tile([P, NQ], U8, name="q_scales", align_bytes=64)
         nc.vector.quantize_mx(
             out=q_codes[:].bitcast(FP8X4), scales=q_scales[:], in_=q_grouped[:].rearrange("p w j -> p (w j)")
         )
 
-        scale_paired = held.tile([P, N], U8, name="scale_paired", align_bytes=64)
-        nc.vector.tensor_copy(
-            scale_paired[:].bitcast(I32).rearrange("p (t s r) -> p t s r", t=2, s=RUNS),
-            scale_listed[:].bitcast(I32).rearrange("p (s t r) -> p t s r", t=2, s=RUNS),
-        )
-        scale_cols = scale_paired[:]
 
-        lq_paired = held.tile([P, N], F32, name="lq_paired", tag="q_then_lq")
-        nc.scalar.activation(
-            lq_paired[:].rearrange("p (t s r) -> p t s r", t=2, s=RUNS),
-            lq_listed[:].rearrange("p (s t r) -> p t s r", t=2, s=RUNS),
-            ACT.Copy,
-        )
-
+        lq_paired = held.tile([P, 2, 2, P], F32, name="lq_paired", tag="q_then_lq")
         lq_turned = psum.tile([P, 4, P], F32, name="lq_turned")
-        for blk in range(4):
-            nc.tensor.transpose(lq_turned[:, blk, :], lq_paired[:, blk * P : (blk + 1) * P], ident[:])
+        for h in range(2):
+            nc.scalar.activation(
+                lq_paired[:, h].rearrange("p t (s r) -> p t s r", r=HALF_RUN),
+                lq_listed[:, h, :].rearrange("p (s t r) -> p t s r", t=2, r=HALF_RUN),
+                ACT.Copy,
+            )
+            for t in range(2):
+                nc.tensor.transpose(lq_turned[:, 2 * t + h, :], lq_paired[:, h, t, :], ident[:])
         lq_col = held.tile([P, 4], F32, name="lq_col")
         nc.scalar.activation(lq_col[:], lq_turned[:, :, P - 1], ACT.Copy)
         knee = held.tile([P, 4], F32, name="knee")
@@ -127,7 +135,7 @@ def tile_attend_nce_topk_kernel(tc, qT, k_words, k_scales, lq, offs, out):
                 scores[h, t] = bank
                 sig[h, t] = s
 
-        terms = held.tile([P, 2, RUNS, PITCH], F32, name="terms")
+        terms = [held.tile([P, 2, RUNS // 2, PITCH], F32, name=f"terms{h}") for h in range(2)]
         turned = []
         excess = []
         for h in range(2):
@@ -151,7 +159,7 @@ def tile_attend_nce_topk_kernel(tc, qT, k_words, k_scales, lq, offs, out):
             excess.append(over_turned)
         for h in range(2):
             nc.vector.tensor_reduce(
-                terms[:, :, h * (RUNS // 2) : (h + 1) * (RUNS // 2), HALF_RUN],
+                terms[h][:, :, :, HALF_RUN],
                 excess[h][:].rearrange("p b (s r) -> p b s r", r=HALF_RUN),
                 AX.X,
                 ALU.add,
@@ -161,9 +169,9 @@ def tile_attend_nce_topk_kernel(tc, qT, k_words, k_scales, lq, offs, out):
         for h in range(2):
             runs = slice(h * (RUNS // 2), (h + 1) * (RUNS // 2))
             nc.scalar.activation(
-                terms[:, :, runs, 0:HALF_RUN],
+                terms[h][:, :, :, 0:HALF_RUN],
                 turned[h][:].rearrange("p b (s r) -> p b s r", r=HALF_RUN),
                 ACT.Ln,
             )
-            nc.vector.tensor_reduce(sums[:, :, runs], terms[:, :, runs, 0 : HALF_RUN + 1], AX.X, ALU.add, negate=True)
+            nc.vector.tensor_reduce(sums[:, :, runs], terms[h][:, :, :, 0 : HALF_RUN + 1], AX.X, ALU.add, negate=True)
         nc.sync.dma_start(out=out[0].rearrange("(b p) r -> p b r", b=2), in_=sums[:])

@@ -91,7 +91,7 @@ def tile_attend_nce_topk_kernel(tc, qT, k_words, k_scales, lq, offs, out):
 
 
         lq_paired = held.tile([P, 2, 2, P], F32, name="lq_paired", tag="q_then_lq")
-        lq_turned = psum.tile([P, 4, P], F32, name="lq_turned")
+        lq_turned = psum.tile([P, 4, P], F32, name="lq_turned", tag="lq_then_product")
         for h in range(2):
             nc.scalar.activation(
                 lq_paired[:, h].rearrange("p t (s r) -> p t s r", r=HALF_RUN),
@@ -100,7 +100,7 @@ def tile_attend_nce_topk_kernel(tc, qT, k_words, k_scales, lq, offs, out):
             )
             for t in range(2):
                 nc.tensor.transpose(lq_turned[:, 2 * t + h, :], lq_paired[:, h, t, :], ident[:])
-        lq_col = held.tile([P, 4], F32, name="lq_col")
+        lq_col = held.tile([P, 4], F32, name="lq_col", tag="bias_then_product")
         nc.scalar.activation(lq_col[:], lq_turned[:, :, P - 1], ACT.Copy)
         knee = held.tile([P, 4], F32, name="knee")
         nc.scalar.activation(knee[:], lq_turned[:, :, P - 1], ACT.Copy, bias=CAP)
@@ -115,63 +115,102 @@ def tile_attend_nce_topk_kernel(tc, qT, k_words, k_scales, lq, offs, out):
                 word_pool[:].bitcast(U32).indirect(offsets[:, 16 * h : 16 * (h + 1)]),
             )
 
-        scores = {}
-        sig = {}
-        for h in range(2):
-            for t in range(2):
-                blk = 2 * t + h
-                bank = psum.tile([P, NQ], F32, name=f"scores{h}{t}", tag=f"bank{h}{t}")
-                nc.tensor.matmul_mx(
-                    out=bank[:],
-                    lhsT=words[:].rearrange("p h t s r -> p h t (s r)")[:, h, t, :].bitcast(FP8X4),
-                    lhsT_scale=scale_cols[:, blk * P : (blk + 1) * P],
-                    rhs=q_codes[:].bitcast(FP8X4),
-                    rhs_scale=q_scales[:],
-                    start=True,
-                    stop=True,
-                )
-                s = held.tile([P, NQ], F32, name=f"sig{h}{t}")
-                nc.scalar.activation(s[:], bank[:], ACT.Sigmoid, bias=lq_col[:, blk : blk + 1], scale=-1.0)
-                scores[h, t] = bank
-                sig[h, t] = s
+        halves = [slice(0, P), slice(P, NQ)]
+        slot_words = words[:].rearrange("p h t s r -> p h t (s r)")
 
-        terms = [held.tile([P, 2, RUNS // 2, PITCH], F32, name=f"terms{h}") for h in range(2)]
-        turned = []
-        excess = []
-        for h in range(2):
-            first = held.tile([P, NQ], F32, name=f"first{h}")
-            nc.vector.tensor_scalar(first[:], sig[h, 0][:], floor[:], None, ALU.max)
-            part = held.tile([P, NQ], F32, name=f"part{h}")
-            nc.vector.tensor_scalar(
-                part[:], scores[h, 0][:], knee[:, h : h + 1], knee_sum[:, h : h + 1], ALU.max, ALU.subtract
+        def score(h, t, cols, bank):
+            blk = 2 * t + h
+            nc.tensor.matmul_mx(
+                out=bank,
+                lhsT=slot_words[:, h, t, :].bitcast(FP8X4),
+                lhsT_scale=scale_cols[:, blk * P : (blk + 1) * P],
+                rhs=q_codes[:, cols].bitcast(FP8X4),
+                rhs_scale=q_scales[:, cols],
+                start=True,
+                stop=True,
             )
-            prod = held.tile([P, NQ], F32, name=f"prod{h}")
-            nc.vector.scalar_tensor_tensor(prod[:], sig[h, 1][:], floor[:], first[:], ALU.max, ALU.mult)
-            over = held.tile([P, NQ], F32, name=f"over{h}")
-            nc.vector.scalar_tensor_tensor(over[:], scores[h, 1][:], knee[:, 2 + h : 3 + h], part[:], ALU.max, ALU.add)
-            prod_turned = psum.tile([P, 2, P], F32, name=f"prod_turned{h}")
+            nc.scalar.activation(sig[h, t][:, cols], bank, ACT.Sigmoid, bias=lq_col[:, blk : blk + 1], scale=-1.0)
+
+        sig = {(h, t): held.tile([P, NQ], F32, name=f"sig{h}{t}") for h in range(2) for t in range(2)}
+        opening = [psum.tile([P, P], F32, name=f"opening{qb}", tag=f"opening{qb}") for qb in range(2)]
+        scores = {ht: psum.tile([P, NQ], F32, name=f"scores{ht[0]}{ht[1]}", tag=f"scores{ht[0]}{ht[1]}") for ht in ((0, 1), (1, 0), (1, 1))}
+        for qb in range(2):
+            score(0, 0, halves[qb], opening[qb][:])
+        for h, t in scores:
+            score(h, t, slice(0, NQ), scores[h, t][:])
+
+        first = [held.tile([P, NQ], F32, name=f"first{h}") for h in range(2)]
+        part = [held.tile([P, NQ], F32, name=f"part{h}") for h in range(2)]
+        prod = [
+            held.tile([P, NQ], F32, name=f"prod{h}", tag=tag) for h, tag in enumerate(("bias_then_product", "prod1"))
+        ]
+        over = [held.tile([P, NQ], F32, name=f"over{h}") for h in range(2)]
+        terms = [held.tile([P, 2, RUNS // 2, PITCH], F32, name=f"terms{h}") for h in range(2)]
+        prod_turned = psum.tile([P, 2, P], F32, name="prod_turned")
+        last_turned = [
+            psum.tile([P, P], F32, name=f"last_turned{qb}", tag=tag) for qb, tag in enumerate(("lq_then_product", "last"))
+        ]
+
+        def floor_first(h):
+            nc.gpsimd.tensor_scalar(first[h][:], sig[h, 0][:], 1.0, floor[:], ALU.min, ALU.max)
+
+        def excess_first(h, cols, bank):
+            nc.vector.tensor_scalar(
+                part[h][:, cols], bank, knee[:, h : h + 1], knee_sum[:, h : h + 1], ALU.max, ALU.subtract
+            )
+
+        def product(h, cols):
+            nc.vector.scalar_tensor_tensor(
+                prod[h][:, cols], sig[h, 1][:, cols], floor[:], first[h][:, cols], ALU.max, ALU.mult
+            )
+
+        def excess_second(h, cols):
+            nc.vector.scalar_tensor_tensor(
+                over[h][:, cols], scores[h, 1][:, cols], knee[:, 2 + h : 3 + h], part[h][:, cols], ALU.max, ALU.add
+            )
+
+        def turn(dst, src):
             for qb in range(2):
-                nc.tensor.transpose(prod_turned[:, qb, :], prod[:, qb * P : (qb + 1) * P], ident[:])
-            over_turned = psum.tile([P, 2, P], F32, name=f"over_turned{h}", tag=f"bank{h}0")
-            for qb in range(2):
-                nc.tensor.transpose(over_turned[:, qb, :], over[:, qb * P : (qb + 1) * P], ident[:])
-            turned.append(prod_turned)
-            excess.append(over_turned)
+                nc.tensor.transpose(dst[:, qb, :], src[:, halves[qb]], ident[:])
+
+        whole = slice(0, NQ)
+        for qb in range(2):
+            excess_first(0, halves[qb], opening[qb][:])
+        floor_first(0)
+        floor_first(1)
+        excess_second(0, whole)
+        excess_first(1, whole, scores[1, 0][:])
+        product(0, whole)
+        over_turned = [
+            psum.tile([P, 2, P], F32, name=f"over_turned{h}", tag=tag) for h, tag in enumerate(("scores10", "opening0"))
+        ]
+        turn(prod_turned, prod[0])
+        turn(over_turned[0], over[0])
+        excess_second(1, whole)
+        turn(over_turned[1], over[1])
+        for qb in range(2):
+            product(1, halves[qb])
+            nc.tensor.transpose(last_turned[qb][:], prod[1][:, halves[qb]], ident[:])
         for h in range(2):
             nc.vector.tensor_reduce(
                 terms[h][:, :, :, HALF_RUN],
-                excess[h][:].rearrange("p b (s r) -> p b s r", r=HALF_RUN),
+                over_turned[h][:].rearrange("p b (s r) -> p b s r", r=HALF_RUN),
                 AX.X,
                 ALU.add,
                 negate=True,
             )
         sums = held.tile([P, 2, RUNS], F32, name="sums")
-        for h in range(2):
-            runs = slice(h * (RUNS // 2), (h + 1) * (RUNS // 2))
+        nc.scalar.activation(
+            terms[0][:, :, :, 0:HALF_RUN], prod_turned[:].rearrange("p b (s r) -> p b s r", r=HALF_RUN), ACT.Ln
+        )
+        nc.vector.tensor_reduce(
+            sums[:, :, 0 : RUNS // 2], terms[0][:, :, :, 0 : HALF_RUN + 1], AX.X, ALU.add, negate=True
+        )
+        for qb in range(2):
             nc.scalar.activation(
-                terms[h][:, :, :, 0:HALF_RUN],
-                turned[h][:].rearrange("p b (s r) -> p b s r", r=HALF_RUN),
-                ACT.Ln,
+                terms[1][:, qb, :, 0:HALF_RUN], last_turned[qb][:].rearrange("p (s r) -> p s r", r=HALF_RUN), ACT.Ln
             )
-            nc.vector.tensor_reduce(sums[:, :, runs], terms[h][:, :, :, 0 : HALF_RUN + 1], AX.X, ALU.add, negate=True)
+            nc.vector.tensor_reduce(
+                sums[:, qb, RUNS // 2 : RUNS], terms[1][:, qb, :, 0 : HALF_RUN + 1], AX.X, ALU.add, negate=True
+            )
         nc.sync.dma_start(out=out[0].rearrange("(b p) r -> p b r", b=2), in_=sums[:])

@@ -23,7 +23,7 @@ RUNS = 16
 HALF_RUN = 16
 CAP = 20.0
 PITCH = 20
-ROW0 = 48
+ROW0 = 112
 FLOPS = 2 * NQ * N * D
 BYTES = D * NQ * 4 + P * T * 4 + 16 * T + T * 4 + P * (N // 16) * 2 + NQ * RUNS * 4
 
@@ -36,12 +36,12 @@ def tile_attend_nce_topk_kernel(tc, qT, k_words, k_scales, lq, offs, out):
 
         offsets = held.tile([P, N // 16], U16, name="offsets")
         lq_pool = held.tile([P, T], F32, name="lq_pool", tag="lq_then_q", align_bytes=64)
-        scale_pool = held.tile([P, T // 4], I32, name="scale_pool", tag="scales_then_lq")
+        scale_pool = held.tile([P, T // 4], I32, name="scale_pool")
         word_pool = held.tile([P, T], I32, name="word_pool")
-        q_raw = held.tile([P, 4, NQ], F32, name="q_raw", tag="q_then_lq")
+        q_raw = held.tile([P, 4, NQ], F32, name="q_raw")
 
         nc.sync.dma_start(offsets[:], offs)
-        nc.sync.dma_start(out=scale_pool[ROW0 : ROW0 + 16, :], in_=k_scales[0].bitcast(I32))
+        nc.scalar.dma_start(out=scale_pool[ROW0 : ROW0 + 16, :], in_=k_scales[0].bitcast(I32))
         nc.scalar.dma_start(out=lq_pool[P - 1 : P, :], in_=lq[0:1, :])
         nc.sync.dma_start(out=q_raw[:], in_=qT[0].rearrange("(p j) w -> p j w", j=4))
         nc.sync.dma_start(out=word_pool[:], in_=k_words[0].rearrange("p t r -> p (t r)").bitcast(I32))
@@ -51,31 +51,31 @@ def tile_attend_nce_topk_kernel(tc, qT, k_words, k_scales, lq, offs, out):
         floor = held.tile([P, 1], F32, name="floor")
         nc.scalar.activation(floor[:], neg_cap[:], ACT.Sigmoid)
 
-        nc.vector.memset(scale_pool[0:ROW0, :], 0)
-        nc.vector.memset(scale_pool[ROW0 + 16 : P, :], 0)
-        scale_plane = held.tile([P, N], U8, name="scale_plane", align_bytes=64)
-        nc.vector.memset(scale_plane[:].bitcast(I32), 0)
-        nc.vector.memset(lq_pool[0 : P - 1, :], 0.0)
         ident = held.tile([P, P], F32, name="ident")
         nc.vector.memset(ident[:], 0.0)
         make_identity(nc, ident[:], nomemset=True)
+        nc.vector.memset(scale_pool[0:ROW0, :], 0)
+        nc.vector.memset(lq_pool[0 : P - 1, :], 0.0)
 
         scale_listed = held.tile([P, N], U8, name="scale_listed")
         nc.vector.tensor_copy(scale_listed[:], scale_pool[:].bitcast(U8).indirect(offsets[:]))
-        scale_paired = held.tile([P, N], U8, name="scale_paired")
+        scale_plane = held.tile([P, N], U8, name="scale_plane", align_bytes=64)
         nc.vector.tensor_copy(
-            scale_paired[:].bitcast(I32).rearrange("p (t s r) -> p t s r", t=2, s=RUNS),
+            scale_plane[:].bitcast(I32).rearrange("p (t s r) -> p t s r", t=2, s=RUNS),
             scale_listed[:].bitcast(I32).rearrange("p (s t r) -> p t s r", t=2, s=RUNS),
         )
         for r in range(4):
             nc.sync.dma_start(
-                out=scale_plane[:].bitcast(I32)[r:P:32, :], in_=scale_paired[:].bitcast(I32)[ROW0 + r : ROW0 + 16 : 4, :]
+                out=scale_plane[:].bitcast(I32)[r:P:32, :], in_=scale_plane[:].bitcast(I32)[ROW0 + r : P : 4, :]
             )
         scale_cols = scale_plane[:]
 
-        lq_listed = held.tile([P, 2, N // 2], F32, name="lq_listed", tag="scales_then_lq")
+        lq_paired = held.tile([P, 2, 2, RUNS // 2, HALF_RUN], U32, name="lq_paired")
         for h in range(2):
-            nc.vector.tensor_copy(lq_listed[:, h, :], lq_pool[:].indirect(offsets[:, 16 * h : 16 * (h + 1)]))
+            nc.vector.tensor_copy(
+                lq_paired[:, h].rearrange("p t s r -> p s t r"),
+                lq_pool[:].bitcast(U32).indirect(offsets[:, 16 * h : 16 * (h + 1)]),
+            )
 
         q_grouped = held.tile([P, NQ, 4], BF16, name="q_grouped", align_bytes=64)
         nc.scalar.activation(
@@ -90,16 +90,11 @@ def tile_attend_nce_topk_kernel(tc, qT, k_words, k_scales, lq, offs, out):
         )
 
 
-        lq_paired = held.tile([P, 2, 2, P], F32, name="lq_paired", tag="q_then_lq")
+        lq_rows = lq_paired[:].rearrange("p h t s r -> p h t (s r)").bitcast(F32)
         lq_turned = psum.tile([P, 4, P], F32, name="lq_turned", tag="lq_then_product")
         for h in range(2):
-            nc.scalar.activation(
-                lq_paired[:, h].rearrange("p t (s r) -> p t s r", r=HALF_RUN),
-                lq_listed[:, h, :].rearrange("p (s t r) -> p t s r", t=2, r=HALF_RUN),
-                ACT.Copy,
-            )
             for t in range(2):
-                nc.tensor.transpose(lq_turned[:, 2 * t + h, :], lq_paired[:, h, t, :], ident[:])
+                nc.tensor.transpose(lq_turned[:, 2 * t + h, :], lq_rows[:, h, t, :], ident[:])
         lq_col = held.tile([P, 4], F32, name="lq_col", tag="bias_then_product")
         nc.scalar.activation(lq_col[:], lq_turned[:, :, P - 1], ACT.Copy)
         knee = held.tile([P, 4], F32, name="knee")

@@ -134,6 +134,18 @@ def tile_attend_nce_topk_kernel(tc, qT, k_words, k_scales, lq, offs, out):
         for h, t in scores:
             score(h, t, slice(0, NQ), scores[h, t][:])
 
+        again = psum.tile([P, NQ], F32, name="again")
+        nc.tensor.matmul_mx(
+            out=again[:],
+            lhsT=slot_words[:, 1, 1, :].bitcast(FP8X4),
+            lhsT_scale=scale_cols[:, 3 * P : 4 * P],
+            rhs=q_codes[:].bitcast(FP8X4),
+            rhs_scale=q_scales[:],
+            start=True,
+            stop=True,
+        )
+        second = (scores[0, 1], again)
+
         first = [held.tile([P, NQ], F32, name=f"first{h}") for h in range(2)]
         part = [held.tile([P, NQ], F32, name=f"part{h}") for h in range(2)]
         prod = [
@@ -143,7 +155,7 @@ def tile_attend_nce_topk_kernel(tc, qT, k_words, k_scales, lq, offs, out):
         terms = [held.tile([P, 2, RUNS // 2, PITCH], F32, name=f"terms{h}") for h in range(2)]
         prod_turned = psum.tile([P, 2, P], F32, name="prod_turned")
         last_turned = [
-            psum.tile([P, P], F32, name=f"last_turned{qb}", tag=tag) for qb, tag in enumerate(("lq_then_product", "last"))
+            psum.tile([P, P], F32, name=f"last_turned{qb}", tag=tag) for qb, tag in enumerate(("lq_then_product", "opening1"))
         ]
 
         def floor_first(h):
@@ -161,7 +173,7 @@ def tile_attend_nce_topk_kernel(tc, qT, k_words, k_scales, lq, offs, out):
 
         def excess_second(h, cols):
             nc.vector.scalar_tensor_tensor(
-                over[h][:, cols], scores[h, 1][:, cols], knee[:, 2 + h : 3 + h], part[h][:, cols], ALU.max, ALU.add
+                over[h][:, cols], second[h][:, cols], knee[:, 2 + h : 3 + h], part[h][:, cols], ALU.max, ALU.add
             )
 
         def turn(dst, src):

@@ -78,10 +78,9 @@ def tile_attend_nce_topk_kernel(tc, qT, k_words, k_scales, lq, offs, out):
             )
 
         q_grouped = held.tile([P, NQ, 4], BF16, name="q_grouped", align_bytes=64)
-        nc.scalar.activation(
-            q_grouped[:].rearrange("p (c i) j -> p c j i", i=4),
-            q_raw[:].rearrange("p j (c i) -> p c j i", i=4),
-            ACT.Copy,
+        nc.scalar.copy(
+            q_grouped[:].rearrange("p (b c m) j -> p c j m b", b=2, m=2),
+            q_raw[:].rearrange("p j (c m b) -> p c j m b", b=2, m=2),
         )
         q_codes = held.tile([P, NQ], U32, name="q_codes", tag="lq_then_q", align_bytes=64)
         q_scales = held.tile([P, NQ], U8, name="q_scales", align_bytes=64)
@@ -220,4 +219,4 @@ def tile_attend_nce_topk_kernel(tc, qT, k_words, k_scales, lq, offs, out):
             nc.vector.tensor_reduce(
                 sums[:, qb, RUNS // 2 : RUNS], terms[1][:, qb, :, 0 : HALF_RUN + 1], AX.X, ALU.add, negate=True
             )
-        nc.sync.dma_start(out=out[0].rearrange("(b p) r -> p b r", b=2), in_=sums[:])
+        nc.sync.dma_start(out=out[0].rearrange("(p b) r -> p b r", b=2), in_=sums[:])

@@ -97,10 +97,11 @@ def tile_attend_nce_topk_kernel(tc, qT, k_words, k_scales, lq, offs, out):
         lq_col = held.tile([P, 4], F32, name="lq_col", tag="bias_then_product")
         nc.scalar.activation(lq_col[:], lq_turned[:, :, P - 1], ACT.Copy)
         knee = held.tile([P, 4], F32, name="knee")
-        nc.scalar.activation(knee[:], lq_turned[:, :, P - 1], ACT.Copy, bias=CAP)
         knee_sum = held.tile([P, 2], F32, name="knee_sum")
         for h in range(2):
-            nc.scalar.activation(knee_sum[:, h : h + 1], knee[:, 2 + h : 3 + h], ACT.Identity, bias=knee[:, h : h + 1])
+            nc.scalar.activation(
+                knee[:, h:4:2], lq_turned[:, h:4:2, P - 1], ACT.Copy, bias=CAP, accum_out=knee_sum[:, h : h + 1]
+            )
 
         words = held.tile([P, 2, 2, RUNS // 2, HALF_RUN], U32, name="words", align_bytes=64)
         for h in range(2):

@@ -94,14 +94,16 @@ def tile_attend_nce_topk_kernel(tc, qT, k_words, k_scales, lq, offs, out):
         for h in range(2):
             for t in range(2):
                 nc.tensor.transpose(lq_turned[:, 2 * t + h, :], lq_rows[:, h, t, :], ident[:])
-        lq_col = held.tile([P, 4], F32, name="lq_col", tag="bias_then_product")
-        nc.scalar.activation(lq_col[:], lq_turned[:, :, P - 1], ACT.Copy)
+        lq_col = [
+            held.tile([P, 2], F32, name=f"lq_col{t}", tag=tag)
+            for t, tag in enumerate(("bias_then_excess", "lq_col1"))
+        ]
+        for t in range(2):
+            nc.scalar.activation(lq_col[t][:], lq_turned[:, 2 * t : 2 * t + 2, P - 1], ACT.Copy)
         knee = held.tile([P, 4], F32, name="knee")
-        knee_sum = held.tile([P, 2], F32, name="knee_sum")
-        for h in range(2):
-            nc.scalar.activation(
-                knee[:, h:4:2], lq_turned[:, h:4:2, P - 1], ACT.Copy, bias=CAP, accum_out=knee_sum[:, h : h + 1]
-            )
+        knee_sum = held.tile([P, 1], F32, name="knee_sum")
+        nc.scalar.activation(knee[:, 0:4:2], lq_turned[:, 0:4:2, P - 1], ACT.Copy, bias=CAP, accum_out=knee_sum[:])
+        nc.scalar.activation(knee[:, 1:4:2], lq_turned[:, 1:4:2, P - 1], ACT.Copy, bias=CAP)
 
         words = held.tile([P, 2, 2, RUNS // 2, HALF_RUN], U32, name="words", align_bytes=64)
         for h in range(2):
@@ -124,7 +126,7 @@ def tile_attend_nce_topk_kernel(tc, qT, k_words, k_scales, lq, offs, out):
                 start=True,
                 stop=True,
             )
-            nc.scalar.activation(sig[h, t][:, cols], bank, ACT.Sigmoid, bias=lq_col[:, blk : blk + 1], scale=-1.0)
+            nc.scalar.activation(sig[h, t][:, cols], bank, ACT.Sigmoid, bias=lq_col[t][:, h : h + 1], scale=-1.0)
 
         sig = {(h, t): held.tile([P, NQ], F32, name=f"sig{h}{t}") for h in range(2) for t in range(2)}
         opening = [psum.tile([P, P], F32, name=f"opening{qb}", tag=f"opening{qb}") for qb in range(2)]
@@ -144,60 +146,58 @@ def tile_attend_nce_topk_kernel(tc, qT, k_words, k_scales, lq, offs, out):
             start=True,
             stop=True,
         )
-        second = (scores[0, 1], again)
 
-        first = [held.tile([P, NQ], F32, name=f"first{h}") for h in range(2)]
+        first = [held.tile([P, NQ], F32, name=f"first{h}", tag=f"first{h}") for h in range(2)]
         part = [held.tile([P, NQ], F32, name=f"part{h}") for h in range(2)]
-        prod = [
-            held.tile([P, NQ], F32, name=f"prod{h}", tag=tag) for h, tag in enumerate(("bias_then_product", "prod1"))
+        prod = [held.tile([P, NQ], F32, name=f"prod{h}") for h in range(2)]
+        over = [
+            held.tile([P, NQ], F32, name=f"over{h}", tag=tag) for h, tag in enumerate(("over0", "bias_then_excess"))
         ]
-        over = [held.tile([P, NQ], F32, name=f"over{h}") for h in range(2)]
-        terms = [held.tile([P, 2, RUNS // 2, PITCH], F32, name=f"terms{h}") for h in range(2)]
         prod_turned = psum.tile([P, 2, P], F32, name="prod_turned")
         last_turned = [
             psum.tile([P, P], F32, name=f"last_turned{qb}", tag=tag) for qb, tag in enumerate(("lq_then_product", "opening1"))
         ]
-
-        def floor_first(h):
-            nc.gpsimd.tensor_scalar(first[h][:], sig[h, 0][:], 1.0, floor[:], ALU.min, ALU.max)
-
-        def excess_first(h, cols, bank):
-            nc.vector.tensor_scalar(
-                part[h][:, cols], bank, knee[:, h : h + 1], knee_sum[:, h : h + 1], ALU.max, ALU.subtract
-            )
 
         def product(h, cols):
             nc.vector.scalar_tensor_tensor(
                 prod[h][:, cols], sig[h, 1][:, cols], floor[:], first[h][:, cols], ALU.max, ALU.mult
             )
 
-        def excess_second(h, cols):
-            nc.vector.scalar_tensor_tensor(
-                over[h][:, cols], second[h][:, cols], knee[:, 2 + h : 3 + h], part[h][:, cols], ALU.max, ALU.add
-            )
-
         def turn(dst, src):
             for qb in range(2):
                 nc.tensor.transpose(dst[:, qb, :], src[:, halves[qb]], ident[:])
 
-        whole = slice(0, NQ)
         for qb in range(2):
-            excess_first(0, halves[qb], opening[qb][:])
-        floor_first(0)
-        floor_first(1)
-        excess_second(0, whole)
-        excess_first(1, whole, scores[1, 0][:])
-        product(0, whole)
+            nc.vector.tensor_scalar(
+                part[0][:, halves[qb]], opening[qb][:], knee[:, 0:1], knee_sum[:], ALU.max, ALU.subtract
+            )
+        nc.vector.tensor_scalar(first[0][:], sig[0, 0][:], floor[:], None, ALU.max)
+        nc.gpsimd.tensor_scalar(first[1][:], sig[1, 0][:], 1.0, floor[:], ALU.min, ALU.max)
+        nc.vector.scalar_tensor_tensor(over[0][:], scores[0, 1][:], knee[:, 2:3], part[0][:], ALU.max, ALU.add)
+        product(0, slice(0, NQ))
+        apart = (part[1], over[1])
+        for t, bank in enumerate((scores[1, 0], again)):
+            bend = knee[:, 2 * t + 1 : 2 * t + 2]
+            nc.vector.tensor_scalar(apart[t][:], bank[:], bend, bend, ALU.max, ALU.subtract)
         over_turned = [
-            psum.tile([P, 2, P], F32, name=f"over_turned{h}", tag=tag) for h, tag in enumerate(("scores10", "opening0"))
+            psum.tile([P, 2, P], F32, name=f"over_turned{h}", tag=tag) for h, tag in enumerate(("scores11", "opening0"))
         ]
         turn(prod_turned, prod[0])
         turn(over_turned[0], over[0])
-        excess_second(1, whole)
-        turn(over_turned[1], over[1])
+        for t in range(2):
+            for qb in range(2):
+                nc.tensor.matmul(
+                    over_turned[1][:, qb, :],
+                    apart[t][:, halves[qb]],
+                    ident[:],
+                    start=(t == 0 and qb == 0),
+                    stop=(t == 1 and qb == 1),
+                    is_transpose=True,
+                )
         for qb in range(2):
             product(1, halves[qb])
             nc.tensor.transpose(last_turned[qb][:], prod[1][:, halves[qb]], ident[:])
+        terms = [held.tile([P, 2, RUNS // 2, PITCH], F32, name=f"terms{h}") for h in range(2)]
         for h in range(2):
             nc.vector.tensor_reduce(
                 terms[h][:, :, :, HALF_RUN],

@@ -1,3 +1,4 @@
+import math
 from contextlib import ExitStack
 
 import concourse.mybir as mybir
@@ -22,6 +23,7 @@ D = 512
 RUNS = 16
 HALF_RUN = 16
 CAP = 20.0
+LIFT = 36.0
 PITCH = 20
 ROW0 = 112
 FLOPS = 2 * NQ * N * D
@@ -103,6 +105,8 @@ def tile_attend_nce_topk_kernel(tc, qT, k_words, k_scales, lq, offs, out):
         knee = held.tile([P, 4], F32, name="knee")
         knee_sum = held.tile([P, 1], F32, name="knee_sum")
         nc.scalar.activation(knee[:, 0:4:2], lq_turned[:, 0:4:2, P - 1], ACT.Copy, bias=CAP, accum_out=knee_sum[:])
+        base = held.tile([P, 1], F32, name="base")
+        nc.scalar.activation(base[:], knee_sum[:], ACT.Copy, bias=-LIFT / 2)
         nc.scalar.activation(knee[:, 1:4:2], lq_turned[:, 1:4:2, P - 1], ACT.Copy, bias=CAP)
 
         words = held.tile([P, 2, 2, RUNS // 2, HALF_RUN], U32, name="words", align_bytes=64)
@@ -147,13 +151,14 @@ def tile_attend_nce_topk_kernel(tc, qT, k_words, k_scales, lq, offs, out):
             stop=True,
         )
 
-        first = [held.tile([P, NQ], F32, name=f"first{h}", tag=f"first{h}") for h in range(2)]
+        first = {1: held.tile([P, NQ], F32, name="first1")}
         part = [held.tile([P, NQ], F32, name=f"part{h}") for h in range(2)]
-        prod = [held.tile([P, NQ], F32, name=f"prod{h}") for h in range(2)]
+        prod = {1: held.tile([P, NQ], F32, name="prod1")}
         over = [
             held.tile([P, NQ], F32, name=f"over{h}", tag=tag) for h, tag in enumerate(("over0", "bias_then_excess"))
         ]
-        prod_turned = psum.tile([P, 2, P], F32, name="prod_turned")
+        floored_turned = psum.tile([P, 2, 2, P], F32, name="floored_turned")
+        floored = [held.tile([P, NQ], F32, name=f"floored{t}") for t in range(2)]
         last_turned = [
             psum.tile([P, P], F32, name=f"last_turned{qb}", tag=tag) for qb, tag in enumerate(("lq_then_product", "opening1"))
         ]
@@ -169,12 +174,12 @@ def tile_attend_nce_topk_kernel(tc, qT, k_words, k_scales, lq, offs, out):
 
         for qb in range(2):
             nc.vector.tensor_scalar(
-                part[0][:, halves[qb]], opening[qb][:], knee[:, 0:1], knee_sum[:], ALU.max, ALU.subtract
+                part[0][:, halves[qb]], opening[qb][:], knee[:, 0:1], base[:], ALU.max, ALU.subtract
             )
-        nc.vector.tensor_scalar(first[0][:], sig[0, 0][:], floor[:], None, ALU.max)
+        nc.vector.tensor_scalar(floored[0][:], sig[0, 0][:], floor[:], None, ALU.max)
+        nc.gpsimd.tensor_scalar(floored[1][:], sig[0, 1][:], 1.0, floor[:], ALU.min, ALU.max)
         nc.gpsimd.tensor_scalar(first[1][:], sig[1, 0][:], 1.0, floor[:], ALU.min, ALU.max)
         nc.vector.scalar_tensor_tensor(over[0][:], scores[0, 1][:], knee[:, 2:3], part[0][:], ALU.max, ALU.add)
-        product(0, slice(0, NQ))
         apart = (part[1], over[1])
         for t, bank in enumerate((scores[1, 0], again)):
             bend = knee[:, 2 * t + 1 : 2 * t + 2]
@@ -182,7 +187,8 @@ def tile_attend_nce_topk_kernel(tc, qT, k_words, k_scales, lq, offs, out):
         over_turned = [
             psum.tile([P, 2, P], F32, name=f"over_turned{h}", tag=tag) for h, tag in enumerate(("scores11", "opening0"))
         ]
-        turn(prod_turned, prod[0])
+        for t in range(2):
+            turn(floored_turned[:, :, t, :], floored[t])
         turn(over_turned[0], over[0])
         for t in range(2):
             for qb in range(2):
@@ -197,10 +203,12 @@ def tile_attend_nce_topk_kernel(tc, qT, k_words, k_scales, lq, offs, out):
         for qb in range(2):
             product(1, halves[qb])
             nc.tensor.transpose(last_turned[qb][:], prod[1][:, halves[qb]], ident[:])
+        fours = held.tile([P, 2, P // 2], F32, name="fours")
+        nc.vector.tensor_reduce(fours[:], floored_turned[:].rearrange("p b t (g e) -> p b g t e", e=2), AX.XY, ALU.mult)
         terms = [held.tile([P, 2, RUNS // 2, PITCH], F32, name=f"terms{h}") for h in range(2)]
         for h in range(2):
             nc.vector.tensor_reduce(
-                terms[h][:, :, :, HALF_RUN],
+                terms[h][:, :, :, (HALF_RUN // 2, HALF_RUN)[h]],
                 over_turned[h][:].rearrange("p b (s r) -> p b s r", r=HALF_RUN),
                 AX.X,
                 ALU.add,
@@ -208,10 +216,13 @@ def tile_attend_nce_topk_kernel(tc, qT, k_words, k_scales, lq, offs, out):
             )
         sums = held.tile([P, 2, RUNS], F32, name="sums")
         nc.scalar.activation(
-            terms[0][:, :, :, 0:HALF_RUN], prod_turned[:].rearrange("p b (s r) -> p b s r", r=HALF_RUN), ACT.Ln
+            terms[0][:, :, :, 0 : HALF_RUN // 2],
+            fours[:].rearrange("p b (s g) -> p b s g", g=HALF_RUN // 2),
+            ACT.Ln,
+            scale=math.exp(LIFT),
         )
         nc.vector.tensor_reduce(
-            sums[:, :, 0 : RUNS // 2], terms[0][:, :, :, 0 : HALF_RUN + 1], AX.X, ALU.add, negate=True
+            sums[:, :, 0 : RUNS // 2], terms[0][:, :, :, 0 : HALF_RUN // 2 + 1], AX.X, ALU.add, negate=True
         )
         for qb in range(2):
             nc.scalar.activation(

@@ -176,10 +176,10 @@ def tile_attend_nce_topk_kernel(tc, qT, k_words, k_scales, lq, offs, out):
             nc.vector.tensor_scalar(
                 part[0][:, halves[qb]], opening[qb][:], knee[:, 0:1], base[:], ALU.max, ALU.subtract
             )
-        nc.vector.tensor_scalar(floored[0][:], sig[0, 0][:], floor[:], None, ALU.max)
-        nc.gpsimd.tensor_scalar(floored[1][:], sig[0, 1][:], 1.0, floor[:], ALU.min, ALU.max)
+        nc.gpsimd.tensor_scalar(floored[0][:], sig[0, 0][:], 1.0, floor[:], ALU.min, ALU.max)
         nc.gpsimd.tensor_scalar(first[1][:], sig[1, 0][:], 1.0, floor[:], ALU.min, ALU.max)
         nc.vector.scalar_tensor_tensor(over[0][:], scores[0, 1][:], knee[:, 2:3], part[0][:], ALU.max, ALU.add)
+        nc.vector.tensor_scalar(floored[1][:], sig[0, 1][:], floor[:], None, ALU.max)
         apart = (part[1], over[1])
         for t, bank in enumerate((scores[1, 0], again)):
             bend = knee[:, 2 * t + 1 : 2 * t + 2]

@@ -22,8 +22,8 @@ NQ = 256
 D = 512
 RUNS = 16
 HALF_RUN = 16
-CAP = 20.0
-LIFT = 36.0
+CAP = 10.75
+LIFT = 43.0
 PITCH = 20
 ROW0 = 112
 FLOPS = 2 * NQ * N * D
@@ -63,13 +63,14 @@ def tile_attend_nce_topk_kernel(tc, qT, k_words, k_scales, lq, offs, out):
         nc.vector.tensor_copy(scale_listed[:], scale_pool[:].bitcast(U8).indirect(offsets[:]))
         scale_plane = held.tile([P, N], U8, name="scale_plane", align_bytes=64)
         nc.vector.tensor_copy(
-            scale_plane[:].bitcast(I32).rearrange("p (t s r) -> p t s r", t=2, s=RUNS),
-            scale_listed[:].bitcast(I32).rearrange("p (s t r) -> p t s r", t=2, s=RUNS),
+            scale_plane[:].bitcast(I32).rearrange("p (h t s r) -> p h t s r", h=2, t=2, s=RUNS // 2),
+            scale_listed[:].bitcast(I32).rearrange("p (h s t r) -> p h t s r", h=2, t=2, s=RUNS // 2),
         )
-        for r in range(4):
-            nc.sync.dma_start(
-                out=scale_plane[:].bitcast(I32)[r:P:32, :], in_=scale_plane[:].bitcast(I32)[ROW0 + r : P : 4, :]
-            )
+        plane_words = scale_plane[:].bitcast(I32)
+        first_half, second_half = slice(0, N // 8), slice(N // 8, N // 4)
+        moves = [(0, slice(0, N // 4))] + [(r, cols) for cols in (first_half, second_half) for r in (1, 2, 3)]
+        for r, cols in moves:
+            nc.sync.dma_start(out=plane_words[r:P:32, cols], in_=plane_words[ROW0 + r : P : 4, cols])
         scale_cols = scale_plane[:]
 
         lq_paired = held.tile([P, 2, 2, RUNS // 2, HALF_RUN], U32, name="lq_paired")
@@ -106,7 +107,7 @@ def tile_attend_nce_topk_kernel(tc, qT, k_words, k_scales, lq, offs, out):
         knee_sum = held.tile([P, 1], F32, name="knee_sum")
         nc.scalar.activation(knee[:, 0:4:2], lq_turned[:, 0:4:2, P - 1], ACT.Copy, bias=CAP, accum_out=knee_sum[:])
         base = held.tile([P, 1], F32, name="base")
-        nc.scalar.activation(base[:], knee_sum[:], ACT.Copy, bias=-LIFT / 2)
+        nc.scalar.activation(base[:], knee_sum[:], ACT.Copy, bias=-LIFT / 4)
         nc.scalar.activation(knee[:, 1:4:2], lq_turned[:, 1:4:2, P - 1], ACT.Copy, bias=CAP)
 
         words = held.tile([P, 2, 2, RUNS // 2, HALF_RUN], U32, name="words", align_bytes=64)
@@ -120,7 +121,7 @@ def tile_attend_nce_topk_kernel(tc, qT, k_words, k_scales, lq, offs, out):
         slot_words = words[:].rearrange("p h t s r -> p h t (s r)")
 
         def score(h, t, cols, bank):
-            blk = 2 * t + h
+            blk = 2 * h + t
             nc.tensor.matmul_mx(
                 out=bank,
                 lhsT=slot_words[:, h, t, :].bitcast(FP8X4),
@@ -203,12 +204,12 @@ def tile_attend_nce_topk_kernel(tc, qT, k_words, k_scales, lq, offs, out):
         for qb in range(2):
             product(1, halves[qb])
             nc.tensor.transpose(last_turned[qb][:], prod[1][:, halves[qb]], ident[:])
-        fours = held.tile([P, 2, P // 2], F32, name="fours")
-        nc.vector.tensor_reduce(fours[:], floored_turned[:].rearrange("p b t (g e) -> p b g t e", e=2), AX.XY, ALU.mult)
+        eights = held.tile([P, 2, P // 4], F32, name="eights")
+        nc.vector.tensor_reduce(eights[:], floored_turned[:].rearrange("p b t (g e) -> p b g t e", e=4), AX.XY, ALU.mult)
         terms = [held.tile([P, 2, RUNS // 2, PITCH], F32, name=f"terms{h}") for h in range(2)]
         for h in range(2):
             nc.vector.tensor_reduce(
-                terms[h][:, :, :, (HALF_RUN // 2, HALF_RUN)[h]],
+                terms[h][:, :, :, (HALF_RUN // 4, HALF_RUN)[h]],
                 over_turned[h][:].rearrange("p b (s r) -> p b s r", r=HALF_RUN),
                 AX.X,
                 ALU.add,
@@ -216,13 +217,13 @@ def tile_attend_nce_topk_kernel(tc, qT, k_words, k_scales, lq, offs, out):
             )
         sums = held.tile([P, 2, RUNS], F32, name="sums")
         nc.scalar.activation(
-            terms[0][:, :, :, 0 : HALF_RUN // 2],
-            fours[:].rearrange("p b (s g) -> p b s g", g=HALF_RUN // 2),
+            terms[0][:, :, :, 0 : HALF_RUN // 4],
+            eights[:].rearrange("p b (s g) -> p b s g", g=HALF_RUN // 4),
             ACT.Ln,
             scale=math.exp(LIFT),
         )
         nc.vector.tensor_reduce(
-            sums[:, :, 0 : RUNS // 2], terms[0][:, :, :, 0 : HALF_RUN // 2 + 1], AX.X, ALU.add, negate=True
+            sums[:, :, 0 : RUNS // 2], terms[0][:, :, :, 0 : HALF_RUN // 4 + 1], AX.X, ALU.add, negate=True
         )
         for qb in range(2):
             nc.scalar.activation(

@@ -59,16 +59,20 @@ def tile_attend_nce_topk_kernel(tc, qT, k_words, k_scales, lq, offs, out):
         nc.vector.memset(scale_pool[0:ROW0, :], 0)
         nc.vector.memset(lq_pool[0 : P - 1, :], 0.0)
 
-        scale_listed = held.tile([P, N], U8, name="scale_listed")
-        nc.vector.tensor_copy(scale_listed[:], scale_pool[:].bitcast(U8).indirect(offsets[:]))
+        scale_listed = [held.tile([P, N // 2], U8, name=f"scale_listed{h}") for h in range(2)]
         scale_plane = held.tile([P, N], U8, name="scale_plane", align_bytes=64)
-        nc.vector.tensor_copy(
-            scale_plane[:].bitcast(I32).rearrange("p (h t s r) -> p h t s r", h=2, t=2, s=RUNS // 2),
-            scale_listed[:].bitcast(I32).rearrange("p (h s t r) -> p h t s r", h=2, t=2, s=RUNS // 2),
-        )
         plane_words = scale_plane[:].bitcast(I32)
-        first_half, second_half = slice(0, N // 8), slice(N // 8, N // 4)
-        moves = [(0, slice(0, N // 4))] + [(r, cols) for cols in (first_half, second_half) for r in (1, 2, 3)]
+        half_cols = [slice(0, N // 8), slice(N // 8, N // 4)]
+        for h in range(2):
+            nc.vector.tensor_copy(
+                scale_listed[h][:], scale_pool[:].bitcast(U8).indirect(offsets[:, 16 * h : 16 * (h + 1)])
+            )
+        for h in range(2):
+            nc.vector.tensor_copy(
+                plane_words[:, half_cols[h]].rearrange("p (t s r) -> p t s r", t=2, s=RUNS // 2),
+                scale_listed[h][:].bitcast(I32).rearrange("p (s t r) -> p t s r", t=2, s=RUNS // 2),
+            )
+        moves = [(r, half_cols[0]) for r in range(3)] + [(3, slice(0, N // 4))] + [(r, half_cols[1]) for r in range(3)]
         for r, cols in moves:
             nc.sync.dma_start(out=plane_words[r:P:32, cols], in_=plane_words[ROW0 + r : P : 4, cols])
         scale_cols = scale_plane[:]
@@ -201,8 +205,8 @@ def tile_attend_nce_topk_kernel(tc, qT, k_words, k_scales, lq, offs, out):
                     stop=(t == 1 and qb == 1),
                     is_transpose=True,
                 )
+        product(1, slice(0, NQ))
         for qb in range(2):
-            product(1, halves[qb])
             nc.tensor.transpose(last_turned[qb][:], prod[1][:, halves[qb]], ident[:])
         eights = held.tile([P, 2, P // 4], F32, name="eights")
         nc.vector.tensor_reduce(eights[:], floored_turned[:].rearrange("p b t (g e) -> p b g t e", e=4), AX.XY, ALU.mult)

@@ -23,6 +23,7 @@ D = 512
 RUNS = 16
 HALF_RUN = 16
 CAP = 10.75
+FLOOR = 1.0 / (1.0 + math.exp(CAP))
 LIFT = 43.0
 PITCH = 20
 ROW0 = 112
@@ -181,8 +182,8 @@ def tile_attend_nce_topk_kernel(tc, qT, k_words, k_scales, lq, offs, out):
             nc.vector.tensor_scalar(
                 part[0][:, halves[qb]], opening[qb][:], knee[:, 0:1], base[:], ALU.max, ALU.subtract
             )
-        nc.gpsimd.tensor_scalar(floored[0][:], sig[0, 0][:], 1.0, floor[:], ALU.min, ALU.max)
-        nc.gpsimd.tensor_scalar(first[1][:], sig[1, 0][:], 1.0, floor[:], ALU.min, ALU.max)
+        nc.gpsimd.tensor_scalar(floored[0][:], sig[0, 0][:], 1.0, FLOOR, ALU.min, ALU.max)
+        nc.gpsimd.tensor_scalar(first[1][:], sig[1, 0][:], 1.0, FLOOR, ALU.min, ALU.max)
         nc.vector.scalar_tensor_tensor(over[0][:], scores[0, 1][:], knee[:, 2:3], part[0][:], ALU.max, ALU.add)
         nc.vector.tensor_scalar(floored[1][:], sig[0, 1][:], floor[:], None, ALU.max)
         apart = (part[1], over[1])

import math
from contextlib import ExitStack

import concourse.mybir as mybir
from concourse.masks import make_identity

F32 = mybir.dt.float32
BF16 = mybir.dt.bfloat16
I32 = mybir.dt.int32
U32 = mybir.dt.uint32
U16 = mybir.dt.uint16
U8 = mybir.dt.uint8
FP8X4 = mybir.dt.float8_e4m3fn_x4
ALU = mybir.AluOpType
ACT = mybir.ActivationFunctionType
AX = mybir.AxisListType

P = 128
T = 2048
N = 512
NQ = 256
D = 512
RUNS = 16
HALF_RUN = 16
CAP = 10.75
FLOOR = 1.0 / (1.0 + math.exp(CAP))
LIFT = 43.0
PITCH = 20
ROW0 = 112
FLOPS = 2 * NQ * N * D
BYTES = D * NQ * 4 + P * T * 4 + 16 * T + T * 4 + P * (N // 16) * 2 + NQ * RUNS * 4


def tile_attend_nce_topk_kernel(tc, qT, k_words, k_scales, lq, offs, out):
    nc = tc.nc
    with ExitStack() as ctx:
        held = ctx.enter_context(tc.tile_pool(name="held", bufs=1))
        psum = ctx.enter_context(tc.psum_pool(name="psum", bufs=1))

        offsets = held.tile([P, N // 16], U16, name="offsets")
        lq_pool = held.tile([P, T], F32, name="lq_pool", tag="lq_then_q", align_bytes=64)
        scale_pool = held.tile([P, T // 4], I32, name="scale_pool")
        word_pool = held.tile([P, T], I32, name="word_pool")
        q_raw = held.tile([P, 4, NQ], F32, name="q_raw")

        nc.sync.dma_start(offsets[:], offs)
        nc.scalar.dma_start(out=scale_pool[ROW0 : ROW0 + 16, :], in_=k_scales[0].bitcast(I32))
        nc.scalar.dma_start(out=lq_pool[P - 1 : P, :], in_=lq[0:1, :])
        nc.sync.dma_start(out=q_raw[:], in_=qT[0].rearrange("(p j) w -> p j w", j=4))
        nc.sync.dma_start(out=word_pool[:], in_=k_words[0].rearrange("p t r -> p (t r)").bitcast(I32))

        neg_cap = held.tile([P, 1], F32, name="neg_cap")
        nc.vector.memset(neg_cap[:], -CAP)
        floor = held.tile([P, 1], F32, name="floor")
        nc.scalar.activation(floor[:], neg_cap[:], ACT.Sigmoid)

        ident = held.tile([P, P], F32, name="ident")
        nc.vector.memset(ident[:], 0.0)
        make_identity(nc, ident[:], nomemset=True)
        nc.vector.memset(scale_pool[0:ROW0, :], 0)
        nc.vector.memset(lq_pool[0 : P - 1, :], 0.0)

        scale_listed = [held.tile([P, N // 2], U8, name=f"scale_listed{h}") for h in range(2)]
        scale_plane = held.tile([P, N], U8, name="scale_plane", align_bytes=64)
        plane_words = scale_plane[:].bitcast(I32)
        half_cols = [slice(0, N // 8), slice(N // 8, N // 4)]
        for h in range(2):
            nc.vector.tensor_copy(
                scale_listed[h][:], scale_pool[:].bitcast(U8).indirect(offsets[:, 16 * h : 16 * (h + 1)])
            )
        for h in range(2):
            nc.vector.tensor_copy(
                plane_words[:, half_cols[h]].rearrange("p (t s r) -> p t s r", t=2, s=RUNS // 2),
                scale_listed[h][:].bitcast(I32).rearrange("p (s t r) -> p t s r", t=2, s=RUNS // 2),
            )
        moves = [(r, half_cols[0]) for r in range(3)] + [(3, slice(0, N // 4))] + [(r, half_cols[1]) for r in range(3)]
        for r, cols in moves:
            nc.sync.dma_start(out=plane_words[r:P:32, cols], in_=plane_words[ROW0 + r : P : 4, cols])
        scale_cols = scale_plane[:]

        lq_paired = held.tile([P, 2, 2, RUNS // 2, HALF_RUN], U32, name="lq_paired")
        for h in range(2):
            nc.vector.tensor_copy(
                lq_paired[:, h].rearrange("p t s r -> p s t r"),
                lq_pool[:].bitcast(U32).indirect(offsets[:, 16 * h : 16 * (h + 1)]),
            )

        q_grouped = held.tile([P, NQ, 4], BF16, name="q_grouped", align_bytes=64)
        nc.scalar.copy(
            q_grouped[:].rearrange("p (b c m) j -> p c j m b", b=2, m=2),
            q_raw[:].rearrange("p j (c m b) -> p c j m b", b=2, m=2),
        )
        q_codes = held.tile([P, NQ], U32, name="q_codes", tag="lq_then_q", align_bytes=64)
        q_scales = held.tile([P, NQ], U8, name="q_scales", align_bytes=64)
        nc.vector.quantize_mx(
            out=q_codes[:].bitcast(FP8X4), scales=q_scales[:], in_=q_grouped[:].rearrange("p w j -> p (w j)")
        )


        lq_rows = lq_paired[:].rearrange("p h t s r -> p h t (s r)").bitcast(F32)
        lq_turned = psum.tile([P, 4, P], F32, name="lq_turned", tag="lq_then_product")
        for h in range(2):
            for t in range(2):
                nc.tensor.transpose(lq_turned[:, 2 * t + h, :], lq_rows[:, h, t, :], ident[:])
        lq_col = [
            held.tile([P, 2], F32, name=f"lq_col{t}", tag=tag)
            for t, tag in enumerate(("bias_then_excess", "lq_col1"))
        ]
        for t in range(2):
            nc.scalar.activation(lq_col[t][:], lq_turned[:, 2 * t : 2 * t + 2, P - 1], ACT.Copy)
        knee = held.tile([P, 4], F32, name="knee")
        knee_sum = held.tile([P, 1], F32, name="knee_sum")
        nc.scalar.activation(knee[:, 0:4:2], lq_turned[:, 0:4:2, P - 1], ACT.Copy, bias=CAP, accum_out=knee_sum[:])
        base = held.tile([P, 1], F32, name="base")
        nc.scalar.activation(base[:], knee_sum[:], ACT.Copy, bias=-LIFT / 4)
        nc.scalar.activation(knee[:, 1:4:2], lq_turned[:, 1:4:2, P - 1], ACT.Copy, bias=CAP)

        words = held.tile([P, 2, 2, RUNS // 2, HALF_RUN], U32, name="words", align_bytes=64)
        for h in range(2):
            nc.vector.tensor_copy(
                words[:, h].rearrange("p t s r -> p s t r"),
                word_pool[:].bitcast(U32).indirect(offsets[:, 16 * h : 16 * (h + 1)]),
            )

        halves = [slice(0, P), slice(P, NQ)]
        slot_words = words[:].rearrange("p h t s r -> p h t (s r)")

        def score(h, t, cols, bank):
            blk = 2 * h + t
            nc.tensor.matmul_mx(
                out=bank,
                lhsT=slot_words[:, h, t, :].bitcast(FP8X4),
                lhsT_scale=scale_cols[:, blk * P : (blk + 1) * P],
                rhs=q_codes[:, cols].bitcast(FP8X4),
                rhs_scale=q_scales[:, cols],
                start=True,
                stop=True,
            )
            nc.scalar.activation(sig[h, t][:, cols], bank, ACT.Sigmoid, bias=lq_col[t][:, h : h + 1], scale=-1.0)

        sig = {(h, t): held.tile([P, NQ], F32, name=f"sig{h}{t}") for h in range(2) for t in range(2)}
        opening = [psum.tile([P, P], F32, name=f"opening{qb}", tag=f"opening{qb}") for qb in range(2)]
        scores = {ht: psum.tile([P, NQ], F32, name=f"scores{ht[0]}{ht[1]}", tag=f"scores{ht[0]}{ht[1]}") for ht in ((0, 1), (1, 0), (1, 1))}
        for qb in range(2):
            score(0, 0, halves[qb], opening[qb][:])
        for h, t in scores:
            score(h, t, slice(0, NQ), scores[h, t][:])

        again = psum.tile([P, NQ], F32, name="again")
        nc.tensor.matmul_mx(
            out=again[:],
            lhsT=slot_words[:, 1, 1, :].bitcast(FP8X4),
            lhsT_scale=scale_cols[:, 3 * P : 4 * P],
            rhs=q_codes[:].bitcast(FP8X4),
            rhs_scale=q_scales[:],
            start=True,
            stop=True,
        )

        first = {1: held.tile([P, NQ], F32, name="first1")}
        part = [held.tile([P, NQ], F32, name=f"part{h}") for h in range(2)]
        prod = {1: held.tile([P, NQ], F32, name="prod1")}
        over = [
            held.tile([P, NQ], F32, name=f"over{h}", tag=tag) for h, tag in enumerate(("over0", "bias_then_excess"))
        ]
        floored_turned = psum.tile([P, 2, 2, P], F32, name="floored_turned")
        floored = [held.tile([P, NQ], F32, name=f"floored{t}") for t in range(2)]
        last_turned = [
            psum.tile([P, P], F32, name=f"last_turned{qb}", tag=tag) for qb, tag in enumerate(("lq_then_product", "opening1"))
        ]

        def product(h, cols):
            nc.vector.scalar_tensor_tensor(
                prod[h][:, cols], sig[h, 1][:, cols], floor[:], first[h][:, cols], ALU.max, ALU.mult
            )

        def turn(dst, src):
            for qb in range(2):
                nc.tensor.transpose(dst[:, qb, :], src[:, halves[qb]], ident[:])

        for qb in range(2):
            nc.vector.tensor_scalar(
                part[0][:, halves[qb]], opening[qb][:], knee[:, 0:1], base[:], ALU.max, ALU.subtract
            )
        nc.gpsimd.tensor_scalar(floored[0][:], sig[0, 0][:], 1.0, FLOOR, ALU.min, ALU.max)
        nc.gpsimd.tensor_scalar(first[1][:], sig[1, 0][:], 1.0, FLOOR, ALU.min, ALU.max)
        nc.vector.scalar_tensor_tensor(over[0][:], scores[0, 1][:], knee[:, 2:3], part[0][:], ALU.max, ALU.add)
        nc.vector.tensor_scalar(floored[1][:], sig[0, 1][:], floor[:], None, ALU.max)
        apart = (part[1], over[1])
        for t, bank in enumerate((scores[1, 0], again)):
            bend = knee[:, 2 * t + 1 : 2 * t + 2]
            nc.vector.tensor_scalar(apart[t][:], bank[:], bend, bend, ALU.max, ALU.subtract)
        over_turned = [
            psum.tile([P, 2, P], F32, name=f"over_turned{h}", tag=tag) for h, tag in enumerate(("scores11", "opening0"))
        ]
        for t in range(2):
            turn(floored_turned[:, :, t, :], floored[t])
        turn(over_turned[0], over[0])
        for t in range(2):
            for qb in range(2):
                nc.tensor.matmul(
                    over_turned[1][:, qb, :],
                    apart[t][:, halves[qb]],
                    ident[:],
                    start=(t == 0 and qb == 0),
                    stop=(t == 1 and qb == 1),
                    is_transpose=True,
                )
        product(1, slice(0, NQ))
        for qb in range(2):
            nc.tensor.transpose(last_turned[qb][:], prod[1][:, halves[qb]], ident[:])
        eights = held.tile([P, 2, P // 4], F32, name="eights")
        nc.vector.tensor_reduce(eights[:], floored_turned[:].rearrange("p b t (g e) -> p b g t e", e=4), AX.XY, ALU.mult)
        terms = [held.tile([P, 2, RUNS // 2, PITCH], F32, name=f"terms{h}") for h in range(2)]
        for h in range(2):
            nc.vector.tensor_reduce(
                terms[h][:, :, :, (HALF_RUN // 4, HALF_RUN)[h]],
                over_turned[h][:].rearrange("p b (s r) -> p b s r", r=HALF_RUN),
                AX.X,
                ALU.add,
                negate=True,
            )
        sums = held.tile([P, 2, RUNS], F32, name="sums")
        nc.scalar.activation(
            terms[0][:, :, :, 0 : HALF_RUN // 4],
            eights[:].rearrange("p b (s g) -> p b s g", g=HALF_RUN // 4),
            ACT.Ln,
            scale=math.exp(LIFT),
        )
        nc.vector.tensor_reduce(
            sums[:, :, 0 : RUNS // 2], terms[0][:, :, :, 0 : HALF_RUN // 4 + 1], AX.X, ALU.add, negate=True
        )
        for qb in range(2):
            nc.scalar.activation(
                terms[1][:, qb, :, 0:HALF_RUN], last_turned[qb][:].rearrange("p (s r) -> p s r", r=HALF_RUN), ACT.Ln
            )
            nc.vector.tensor_reduce(
                sums[:, qb, RUNS // 2 : RUNS], terms[1][:, qb, :, 0 : HALF_RUN + 1], AX.X, ALU.add, negate=True
            )
        nc.sync.dma_start(out=out[0].rearrange("(p b) r -> p b r", b=2), in_=sums[:])
